import numpy as np
import ml_dtypes


def mxq(x, axis, fmt="e4m3"):
    dtype, down = {"e4m3": (ml_dtypes.float8_e4m3fn, 7), "e5m2": (ml_dtypes.float8_e5m2, 14)}[fmt]
    v = np.moveaxis(np.asarray(x, np.float32).astype(ml_dtypes.bfloat16).astype(np.float64), axis, -1)
    blocks = v.reshape(v.shape[:-1] + (-1, 32))
    amax = np.abs(blocks).max(-1, keepdims=True)
    byte = np.maximum(np.where(amax > 0, np.frexp(amax)[1] - 1 + 127, 0) - down, 1)
    scale = np.exp2(byte - 127.0)
    codes = (blocks / scale).astype(np.float32).astype(dtype).astype(np.float64)
    return np.moveaxis((codes * scale).reshape(v.shape), -1, axis)


WIDE = False


def mx_kscale(k):
    if not WIDE:
        return np.ones(k)
    levels = np.array([10, -10, 5, -5, 0])
    if k % 512:
        return np.exp2(np.random.permutation(np.resize(levels, k // 32))).repeat(32)
    a = np.empty((k // 512, 16))
    for p in range(k // 512):
        a[p, :8] = np.random.permutation(np.resize(levels, 8))
        for g in range(8):
            far = levels[np.abs(levels - a[p, g]) >= 10]
            a[p, g + 8] = far[np.random.randint(len(far))]
    return np.exp2(a.ravel()).repeat(32)


def f64(x):
    return np.asarray(x).astype(np.float64)


def striped(idx):
    return np.tile(np.asarray(idx).reshape(-1, 16).T, (8, 1)).astype(np.uint16)


def unstriped(offs):
    return offs[:16].T.reshape(-1).astype(np.int64)


def striped8(idx):
    return np.asarray(idx).reshape(8, -1, 16).transpose(0, 2, 1).reshape(128, -1).astype(np.uint16)


def unstriped8(offs):
    return offs.reshape(8, 16, -1).transpose(0, 2, 1).reshape(8, -1).astype(np.int64)


def pick8(x, idx, run):
    r = np.arange(len(x))
    return x[r[:, None], idx[r % (8 * run) // run]]


E2M1 = np.array([0.0, 0.5, 1.0, 1.5, 2.0, 3.0, 4.0, 6.0, -0.0, -0.5, -1.0, -1.5, -2.0, -3.0, -4.0, -6.0])


def pack_weight(w, fmt):
    k, n = w.shape
    w = f64(np.asarray(w, np.float32).astype(ml_dtypes.bfloat16)).reshape(k // 32, 32, n)
    amax = np.abs(w).max(1)
    if fmt == "e4m3":
        byte = np.frexp(amax)[1] - 1 + 127 - 7
    else:
        mant, ex = np.frexp(amax / 6.0)
        byte = np.where(mant > 0.5, ex, ex - 1) + 127
    byte = np.clip(np.where(amax > 0, byte, 1), 1, 254)
    scaled = (w * np.exp2(127.0 - byte)[:, None, :]).reshape(k, n).astype(np.float32)
    by_word = np.ascontiguousarray(scaled.reshape(k // 512, 128, 4, n).transpose(0, 1, 3, 2))
    if fmt == "e4m3":
        words = by_word.astype(ml_dtypes.float8_e4m3fn).view(np.uint8)
    else:
        c = by_word.astype(ml_dtypes.float4_e2m1fn).view(np.uint8) & 0xF
        words = (c[..., 0::2] | (c[..., 1::2] << 4)).reshape(k // 512, 128, 2 * n)
    return np.ascontiguousarray(words), np.ascontiguousarray(byte.astype(np.uint8).reshape(k // 512, 16, n))


def unpack_weight(words, scales, fmt):
    g, _, n = scales.shape
    words = np.ascontiguousarray(words).reshape(g, 128, n, -1)
    if fmt == "e4m3":
        vals = words.view(ml_dtypes.float8_e4m3fn).astype(np.float64)
    else:
        nib = np.empty((g, 128, n, 4), np.uint8)
        nib[..., 0::2] = words & 0xF
        nib[..., 1::2] = words >> 4
        vals = E2M1[nib]
    vals = vals * np.repeat(np.exp2(scales.astype(np.float64) - 127.0), 8, axis=1)[..., None]
    return vals.transpose(0, 1, 3, 2).reshape(g * 512, n)


def sigmoid(v):
    return 1.0 / (1.0 + np.exp(-v))


K, R, F, T, J, M = 512, 128, 512, 2048, 512, 256


def setup_inputs():
    n = np.random.standard_normal
    idx = np.random.permutation(T)[:J]
    idx2 = np.stack([np.random.permutation(J)[:M] for _ in range(8)])
    fk = mx_kscale(K)
    tabp = pack_weight(n((K, T)) / fk[:, None], "e4m3")
    dtabp = pack_weight(n((K, T)) / fk[:, None], "e4m3")
    return {
        "tab_words": tabp[0],
        "tab_scales": tabp[1],
        "dtab_words": dtabp[0],
        "dtab_scales": dtabp[1],
        "w1": (n((K, R)) * 1 / np.sqrt(K) * fk[:, None]).astype(np.float32),
        "bias": (np.random.uniform(-0.5, 0.5, (R, 1))).astype(np.float32),
        "gain": (np.random.uniform(0.5, 1.5, (R, 1))).astype(np.float32),
        "pw": (np.random.uniform(0.5, 1.5, (1, M))).astype(np.float32),
        "og": (np.random.uniform(0.5, 2.0, (R, 1))).astype(np.float32),
        "base": (0.3 * n((R, M))).astype(np.float32),
        "offs": striped(idx),
        "offs2": striped8(idx2),
    }


def reference(tab_words, tab_scales, dtab_words, dtab_scales, w1, bias, gain, pw, og, base, offs, offs2):
    idx = unstriped(offs)
    idx2 = unstriped8(offs2)
    tabu = unpack_weight(tab_words, tab_scales, "e4m3")
    dtabu = unpack_weight(dtab_words, dtab_scales, "e4m3")
    w1q = mxq(f64(w1), 0, "e4m3")
    tabidxg = tabu[:, idx]
    a = w1q.T @ tabidxg
    dtabidxg = dtabu[:, idx]
    ta = w1q.T @ dtabidxg
    h1 = np.tanh(a + f64(bias))
    h2 = h1 * f64(gain)
    s = pick8(h2, idx2, 16) * f64(pw)
    th1 = ta * (1.0 - np.square(h1))
    th2 = th1 * f64(gain)
    ts = pick8(th2, idx2, 16) * f64(pw)
    tu1 = ts * sigmoid(s) * (1.0 + s * (1.0 - sigmoid(s)))
    y = tu1 * f64(og) + f64(base)
    return y

@@ -1,0 +1,148 @@
+from contextlib import ExitStack
+
+import concourse.mybir as mybir
+
+K, R, T, J, M = 512, 128, 2048, 512, 256
+FLOPS = 2 * 2 * K * R * J
+
+F32 = mybir.dt.float32
+BF16 = mybir.dt.bfloat16
+I32 = mybir.dt.int32
+U32 = mybir.dt.uint32
+U16 = mybir.dt.uint16
+U8 = mybir.dt.uint8
+FP8X4 = mybir.dt.float8_e4m3fn_x4
+ACT = mybir.ActivationFunctionType
+ALU = mybir.AluOpType
+
+P = 128
+HALF = J // 2
+
+
+def tile_attend_tcpick_kernel(tc, tab_words, tab_scales, dtab_words, dtab_scales, w1, bias, gain, pw, og, base, offs, offs2, out):
+    nc = tc.nc
+    with ExitStack() as ctx:
+        sb = ctx.enter_context(tc.tile_pool(name="sb", bufs=1))
+        ps = ctx.enter_context(tc.psum_pool(name="ps", bufs=1))
+
+        slots = sb.tile([P, J // 16], U16, name="slots")
+        picks = sb.tile([P, M // 16], U16, name="picks")
+        w_raw = sb.tile([P, 4, R], F32, name="w_raw")
+        tab_s = sb.tile([P, T], U8, name="tab_s")
+        late = ctx.enter_context(tc.tile_pool(name="late", bufs=1))
+        zeros = late.tile([P, 4896], F32, name="zeros", offset=0)
+        nc.vector.memset(tab_s[:].bitcast(I32), 0)
+        nc.vector.memset(zeros[:, :P], 0.0)
+        ident = sb.tile([P, P], F32, name="ident")
+        nc.gpsimd.affine_select(
+            out=ident[:], in_=zeros[:, :P], compare_op=ALU.not_equal, fill=1.0, base=0, pattern=[[-1, P]], channel_multiplier=1
+        )
+        tab_w = late.tile([P, T], I32, name="tab_w", offset=0)
+        dtab_w = late.tile([P, T], I32, name="dtab_w", offset=8192)
+        dtab_s = late.tile([P, T], U8, name="dtab_s", offset=16384)
+        base_sb = late.tile([P, M], F32, name="base_sb", offset=18432)
+        pw_col = late.tile([P, 2], F32, name="pw_col", offset=19456)
+        og_col = late.tile([P, 1], F32, name="og_col", offset=19488)
+        bias_col = late.tile([P, 1], F32, name="bias_col", offset=19520)
+        gain_col = late.tile([P, 1], F32, name="gain_col", offset=19552)
+
+        nc.vector.memset(dtab_s[:].bitcast(I32), 0)
+
+        warm_in = sb.tile([P, 1], F32, name="warm_in")
+        warm_out = sb.tile([P, 1], F32, name="warm_out")
+        nc.gpsimd.memset(warm_in[:], 0.0)
+        nc.scalar.activation(warm_out[:], warm_in[:], ACT.Silu)
+
+        def load_scales(plane, first, scales):
+            rows = scales[0].bitcast(I32).rearrange("(q r) c -> r q c", r=4)
+            for r in range(4):
+                nc.sync.dma_start(plane[first + r : P : 32, :].bitcast(I32), rows[r])
+
+        def load_words(tile, words):
+            nc.sync.dma_start(tile[:], words[0].rearrange("p n t -> p (n t)").bitcast(I32))
+
+        nc.sync.dma_start(slots[:], offs)
+        nc.sync.dma_start(w_raw[:], w1.rearrange("(p j) r -> p j r", j=4))
+        nc.sync.dma_start(picks[:], offs2)
+        load_scales(tab_s, 0, tab_scales)
+        load_words(tab_w, tab_words)
+        nc.sync.dma_start(bias_col[:], bias)
+        load_scales(dtab_s, 4, dtab_scales)
+        load_words(dtab_w, dtab_words)
+        nc.sync.dma_start(base_sb[:], base)
+        nc.sync.dma_start(og_col[:], og)
+
+        nc.gpsimd.dma_start(pw_col[:], pw[0].rearrange("(p h) -> p h", h=2))
+        nc.gpsimd.dma_start(gain_col[:], gain)
+
+        w_bf = sb.tile([P, R, 4], BF16, name="w_bf", align_bytes=64)
+        nc.scalar.copy(w_bf[:], w_raw[:].rearrange("p j r -> p r j"))
+        w_codes = sb.tile([P, R], U32, name="w_codes", align_bytes=64)
+        w_scales = sb.tile([P, R], U8, name="w_scales", align_bytes=64)
+        nc.vector.quantize_mx(out=w_codes[:].bitcast(FP8X4), scales=w_scales[:], in_=w_bf[:].rearrange("p r j -> p (r j)"))
+
+        pw_ps = ps.tile([P, 2, P], F32, name="pw_ps", tag="a0")
+        for h in range(2):
+            nc.tensor.transpose(pw_ps[:, h, :], pw_col[:, h : h + 1].to_broadcast([P, P]), ident[:])
+        pw_row = sb.tile([P, M], F32, name="pw_row")
+        nc.scalar.copy(pw_row[:].rearrange("i (p h) -> i p h", h=2), pw_ps[:].rearrange("i h p -> i p h"))
+        gain_neg = sb.tile([P, 1], F32, name="gain_neg")
+        nc.gpsimd.tensor_scalar(gain_neg[:], gain_col[:], -1.0, 0.0, ALU.mult, ALU.add)
+        og_neg_half = sb.tile([P, 1], F32, name="og_neg_half")
+        nc.gpsimd.tensor_scalar(og_neg_half[:], og_col[:], -0.5, 0.0, ALU.mult, ALU.add)
+
+        def gather_scales(plane, name):
+            got = sb.tile([P, J], U8, name=name, align_bytes=64)
+            nc.vector.tensor_copy(got[:], plane[:].indirect(slots[:]))
+            return got
+
+        def product(tile, got_scales, first, h, name):
+            got = sb.tile([P, HALF], U32, name=name + "_got", align_bytes=64)
+            nc.vector.tensor_copy(got[:], tile[:].bitcast(U32).indirect(slots[:, h * HALF // 16 : (h + 1) * HALF // 16]))
+            acc = ps.tile([P, HALF], F32, name=name, tag=name)
+            nc.tensor.matmul_mx(
+                out=acc[:],
+                lhsT=w_codes[:].bitcast(FP8X4),
+                lhsT_scale=w_scales[:],
+                rhs=got[:].bitcast(FP8X4),
+                rhs_scale=got_scales[first:P, h * HALF : (h + 1) * HALF],
+                start=True,
+                stop=True,
+            )
+            return acc
+
+        h1 = sb.tile([P, J], F32, name="h1")
+        h2 = sb.tile([P, J], F32, name="h2")
+        tab_sg = gather_scales(tab_s, "tab_sg")
+        for h in range(2):
+            cols = slice(h * HALF, (h + 1) * HALF)
+            a = product(tab_w, tab_sg, 0, h, "a%d" % h)
+            nc.scalar.activation(h1[:, cols], a[:], ACT.Tanh, bias=bias_col[:])
+            nc.scalar.activation(h2[:, cols], h1[:, cols], ACT.Copy, scale=gain_col[:])
+        dtab_sg = gather_scales(dtab_s, "dtab_sg")
+
+        s = late.tile([P, M], F32, name="s", offset=16384)
+        nc.vector.tensor_tensor(s[:], h2[:].indirect(picks[:]), pw_row[:], ALU.mult)
+        sq = sb.tile([P, J], F32, name="sq")
+        nc.scalar.activation(sq[:], h1[:], ACT.Square)
+        silu_neg = sb.tile([P, M], F32, name="silu_neg")
+        nc.scalar.activation(silu_neg[:], s[:], ACT.Silu, scale=-1.0)
+        slope = sb.tile([P, J], F32, name="slope")
+        nc.scalar.activation(slope[:], sq[:], ACT.Identity, bias=gain_col[:], scale=gain_neg[:])
+        tanh_half = sb.tile([P, M], F32, name="tanh_half")
+        nc.scalar.activation(tanh_half[:], s[:], ACT.Tanh, scale=0.5)
+
+        ta = [product(dtab_w, dtab_sg, 4, h, "ta%d" % h) for h in range(2)]
+        v = late.tile([P, M], F32, name="v", offset=8192)
+        nc.vector.scalar_tensor_tensor(v[:], silu_neg[:], 1.0, pw_row[:], ALU.subtract, ALU.mult)
+        th2 = sb.tile([P, J], F32, name="th2")
+        for h in range(2):
+            cols = slice(h * HALF, (h + 1) * HALF)
+            nc.vector.tensor_tensor(th2[:, cols], ta[h][:], slope[:, cols], ALU.mult)
+        factor = sb.tile([P, M], F32, name="factor")
+        nc.vector.scalar_tensor_tensor(factor[:], tanh_half[:], 1.0, v[:], ALU.add, ALU.mult)
+        picked = sb.tile([P, M], F32, name="picked")
+        nc.vector.tensor_tensor(picked[:], th2[:].indirect(picks[:]), factor[:], ALU.mult)
+        res = sb.tile([P, M], F32, name="res")
+        nc.vector.scalar_tensor_tensor(res[:], picked[:], og_neg_half[:], base_sb[:], ALU.mult, ALU.add)
+        nc.sync.dma_start(out, res[:])

@@ -27,31 +27,27 @@ def tile_attend_tcpick_kernel(tc, tab_words, tab_scales, dtab_words, dtab_scales
 
         slots = sb.tile([P, J // 16], U16, name="slots")
         picks = sb.tile([P, M // 16], U16, name="picks")
-        w_raw = sb.tile([P, 4, R], F32, name="w_raw")
         tab_s = sb.tile([P, T], U8, name="tab_s")
         late = ctx.enter_context(tc.tile_pool(name="late", bufs=1))
-        zeros = late.tile([P, 4896], F32, name="zeros", offset=0)
+        zeros = late.tile([P, 3224], F32, name="zeros", offset=0)
+        w_raw = late.tile([P, 4, R], F32, name="w_raw", offset=14880)
+        nc.gpsimd.iota(zeros[:, :P].bitcast(I32), pattern=[[1, P]], base=0, channel_multiplier=-1)
         nc.vector.memset(tab_s[:].bitcast(I32), 0)
-        nc.vector.memset(zeros[:, :P], 0.0)
+        warm_in = sb.tile([P, 1], F32, name="warm_in")
+        warm_out = sb.tile([P, 1], F32, name="warm_out")
+        nc.vector.memset(warm_in[:], 0.0)
+        nc.scalar.activation(warm_out[:], warm_in[:], ACT.Silu)
         ident = sb.tile([P, P], F32, name="ident")
-        nc.gpsimd.affine_select(
-            out=ident[:], in_=zeros[:, :P], compare_op=ALU.not_equal, fill=1.0, base=0, pattern=[[-1, P]], channel_multiplier=1
-        )
+        nc.vector.tensor_scalar(ident[:], zeros[:, :P].bitcast(I32), 0.0, None, ALU.is_equal)
         tab_w = late.tile([P, T], I32, name="tab_w", offset=0)
-        dtab_w = late.tile([P, T], I32, name="dtab_w", offset=8192)
-        dtab_s = late.tile([P, T], U8, name="dtab_s", offset=16384)
-        base_sb = late.tile([P, M], F32, name="base_sb", offset=18432)
-        pw_col = late.tile([P, 2], F32, name="pw_col", offset=19456)
-        og_col = late.tile([P, 1], F32, name="og_col", offset=19488)
-        bias_col = late.tile([P, 1], F32, name="bias_col", offset=19520)
-        gain_col = late.tile([P, 1], F32, name="gain_col", offset=19552)
+        dtab_s = late.tile([P, T], U8, name="dtab_s", offset=8192)
+        pw_col = sb.tile([P, 2], F32, name="pw_col")
+        bias_col = late.tile([P, 1], F32, name="bias_col", offset=10240)
+        gain_tile = late.tile([P, 16], F32, name="gain_tile", offset=11808)
+        gain_col = gain_tile[:, 0:1]
 
         nc.vector.memset(dtab_s[:].bitcast(I32), 0)
 
-        warm_in = sb.tile([P, 1], F32, name="warm_in")
-        warm_out = sb.tile([P, 1], F32, name="warm_out")
-        nc.gpsimd.memset(warm_in[:], 0.0)
-        nc.scalar.activation(warm_out[:], warm_in[:], ACT.Silu)
 
         def load_scales(plane, first, scales):
             rows = scales[0].bitcast(I32).rearrange("(q r) c -> r q c", r=4)
@@ -67,37 +63,38 @@ def tile_attend_tcpick_kernel(tc, tab_words, tab_scales, dtab_words, dtab_scales
         load_scales(tab_s, 0, tab_scales)
         load_words(tab_w, tab_words)
         nc.sync.dma_start(bias_col[:], bias)
+        nc.sync.dma_start(gain_col, gain)
         load_scales(dtab_s, 4, dtab_scales)
-        load_words(dtab_w, dtab_words)
-        nc.sync.dma_start(base_sb[:], base)
-        nc.sync.dma_start(og_col[:], og)
 
         nc.gpsimd.dma_start(pw_col[:], pw[0].rearrange("(p h) -> p h", h=2))
-        nc.gpsimd.dma_start(gain_col[:], gain)
 
-        w_bf = sb.tile([P, R, 4], BF16, name="w_bf", align_bytes=64)
+        w_bf = late.tile([P, R, 4], BF16, name="w_bf", align_bytes=64, offset=12864)
         nc.scalar.copy(w_bf[:], w_raw[:].rearrange("p j r -> p r j"))
         w_codes = sb.tile([P, R], U32, name="w_codes", align_bytes=64)
         w_scales = sb.tile([P, R], U8, name="w_scales", align_bytes=64)
         nc.vector.quantize_mx(out=w_codes[:].bitcast(FP8X4), scales=w_scales[:], in_=w_bf[:].rearrange("p r j -> p (r j)"))
 
+        dtab_w = late.tile([P, T], I32, name="dtab_w", offset=14944)
+        base_sb = late.tile([P, M], F32, name="base_sb", offset=13888)
+        og_col = late.tile([P, 1], F32, name="og_col", offset=14912)
+        load_words(dtab_w, dtab_words)
+        nc.sync.dma_start(base_sb[:], base)
+        nc.sync.dma_start(og_col[:], og)
         pw_ps = ps.tile([P, 2, P], F32, name="pw_ps", tag="a0")
         for h in range(2):
             nc.tensor.transpose(pw_ps[:, h, :], pw_col[:, h : h + 1].to_broadcast([P, P]), ident[:])
         pw_row = sb.tile([P, M], F32, name="pw_row")
         nc.scalar.copy(pw_row[:].rearrange("i (p h) -> i p h", h=2), pw_ps[:].rearrange("i h p -> i p h"))
         gain_neg = sb.tile([P, 1], F32, name="gain_neg")
-        nc.gpsimd.tensor_scalar(gain_neg[:], gain_col[:], -1.0, 0.0, ALU.mult, ALU.add)
+        nc.gpsimd.tensor_scalar(gain_neg[:], gain_col, -1.0, 0.0, ALU.mult, ALU.add)
         og_neg_half = sb.tile([P, 1], F32, name="og_neg_half")
         nc.gpsimd.tensor_scalar(og_neg_half[:], og_col[:], -0.5, 0.0, ALU.mult, ALU.add)
 
-        def gather_scales(plane, name):
-            got = sb.tile([P, J], U8, name=name, align_bytes=64)
+        def gather_scales(plane, got):
             nc.vector.tensor_copy(got[:], plane[:].indirect(slots[:]))
             return got
 
-        def product(tile, got_scales, first, h, name):
-            got = sb.tile([P, HALF], U32, name=name + "_got", align_bytes=64)
+        def product(tile, got_scales, first, h, name, got):
             nc.vector.tensor_copy(got[:], tile[:].bitcast(U32).indirect(slots[:, h * HALF // 16 : (h + 1) * HALF // 16]))
             acc = ps.tile([P, HALF], F32, name=name, tag=name)
             nc.tensor.matmul_mx(
@@ -113,36 +110,38 @@ def tile_attend_tcpick_kernel(tc, tab_words, tab_scales, dtab_words, dtab_scales
 
         h1 = sb.tile([P, J], F32, name="h1")
         h2 = sb.tile([P, J], F32, name="h2")
-        tab_sg = gather_scales(tab_s, "tab_sg")
+        tab_sg = gather_scales(tab_s, late.tile([P, J], U8, name="tab_sg", align_bytes=64, offset=10304))
         for h in range(2):
             cols = slice(h * HALF, (h + 1) * HALF)
-            a = product(tab_w, tab_sg, 0, h, "a%d" % h)
+            a = product(tab_w, tab_sg, 0, h, "a%d" % h, sb.tile([P, HALF], U32, name="a_got%d" % h, align_bytes=64))
             nc.scalar.activation(h1[:, cols], a[:], ACT.Tanh, bias=bias_col[:])
-            nc.scalar.activation(h2[:, cols], h1[:, cols], ACT.Copy, scale=gain_col[:])
-        dtab_sg = gather_scales(dtab_s, "dtab_sg")
+            nc.scalar.activation(h2[:, cols], h1[:, cols], ACT.Copy, scale=gain_col)
+        dtab_sg = gather_scales(dtab_s, sb.tile([P, J], U8, name="dtab_sg", align_bytes=64))
 
-        s = late.tile([P, M], F32, name="s", offset=16384)
+        s = late.tile([P, M], F32, name="s", offset=8192)
         nc.vector.tensor_tensor(s[:], h2[:].indirect(picks[:]), pw_row[:], ALU.mult)
         sq = sb.tile([P, J], F32, name="sq")
         nc.scalar.activation(sq[:], h1[:], ACT.Square)
+        slope = sb.tile([P, J], F32, name="slope")
+        nc.scalar.activation(slope[:], sq[:], ACT.Copy, bias=-1.0)
         silu_neg = sb.tile([P, M], F32, name="silu_neg")
         nc.scalar.activation(silu_neg[:], s[:], ACT.Silu, scale=-1.0)
-        slope = sb.tile([P, J], F32, name="slope")
-        nc.scalar.activation(slope[:], sq[:], ACT.Identity, bias=gain_col[:], scale=gain_neg[:])
         tanh_half = sb.tile([P, M], F32, name="tanh_half")
         nc.scalar.activation(tanh_half[:], s[:], ACT.Tanh, scale=0.5)
 
-        ta = [product(dtab_w, dtab_sg, 4, h, "ta%d" % h) for h in range(2)]
-        v = late.tile([P, M], F32, name="v", offset=8192)
+        ta = [product(dtab_w, dtab_sg, 4, h, "ta%d" % h, late.tile([P, HALF], U32, name="ta_got%d" % h, align_bytes=64, offset=10816 + 1024 * h)) for h in range(2)]
+        v = late.tile([P, M], F32, name="v", offset=10816)
         nc.vector.scalar_tensor_tensor(v[:], silu_neg[:], 1.0, pw_row[:], ALU.subtract, ALU.mult)
         th2 = sb.tile([P, J], F32, name="th2")
-        for h in range(2):
-            cols = slice(h * HALF, (h + 1) * HALF)
-            nc.vector.tensor_tensor(th2[:, cols], ta[h][:], slope[:, cols], ALU.mult)
+        nc.vector.scalar_tensor_tensor(th2[:, :HALF], ta[0][:], gain_neg[:], slope[:, :HALF], ALU.mult, ALU.mult)
         factor = sb.tile([P, M], F32, name="factor")
         nc.vector.scalar_tensor_tensor(factor[:], tanh_half[:], 1.0, v[:], ALU.add, ALU.mult)
+        nc.vector.scalar_tensor_tensor(th2[:, HALF:], ta[1][:], gain_neg[:], slope[:, HALF:], ALU.mult, ALU.mult)
         picked = sb.tile([P, M], F32, name="picked")
-        nc.vector.tensor_tensor(picked[:], th2[:].indirect(picks[:]), factor[:], ALU.mult)
         res = sb.tile([P, M], F32, name="res")
-        nc.vector.scalar_tensor_tensor(res[:], picked[:], og_neg_half[:], base_sb[:], ALU.mult, ALU.add)
-        nc.sync.dma_start(out, res[:])
+        halves = [slice(h * M // 2, (h + 1) * M // 2) for h in range(2)]
+        for h, cols in enumerate(halves):
+            nc.vector.tensor_tensor(picked[:, cols], th2[:].indirect(picks[:, 8 * h : 8 * h + 8]), factor[:, cols], ALU.mult)
+        for queue, cols in zip((nc.scalar, nc.sync), halves):
+            nc.vector.scalar_tensor_tensor(res[:, cols], picked[:, cols], og_neg_half[:], base_sb[:, cols], ALU.mult, ALU.add)
+            queue.dma_start(out[:, cols], res[:, cols])

@@ -66,7 +66,7 @@ def tile_attend_tcpick_kernel(tc, tab_words, tab_scales, dtab_words, dtab_scales
         nc.sync.dma_start(gain_col, gain)
         load_scales(dtab_s, 4, dtab_scales)
 
-        nc.gpsimd.dma_start(pw_col[:], pw[0].rearrange("(p h) -> p h", h=2))
+        nc.scalar.dma_start(pw_col[:], pw[0].rearrange("(p h) -> p h", h=2))
 
         w_bf = late.tile([P, R, 4], BF16, name="w_bf", align_bytes=64, offset=12864)
         nc.scalar.copy(w_bf[:], w_raw[:].rearrange("p j r -> p r j"))

from contextlib import ExitStack

import concourse.mybir as mybir

K, R, T, J, M = 512, 128, 2048, 512, 256
FLOPS = 2 * 2 * K * R * J

F32 = mybir.dt.float32
BF16 = mybir.dt.bfloat16
I32 = mybir.dt.int32
U32 = mybir.dt.uint32
U16 = mybir.dt.uint16
U8 = mybir.dt.uint8
FP8X4 = mybir.dt.float8_e4m3fn_x4
ACT = mybir.ActivationFunctionType
ALU = mybir.AluOpType

P = 128
HALF = J // 2


def tile_attend_tcpick_kernel(tc, tab_words, tab_scales, dtab_words, dtab_scales, w1, bias, gain, pw, og, base, offs, offs2, out):
    nc = tc.nc
    with ExitStack() as ctx:
        sb = ctx.enter_context(tc.tile_pool(name="sb", bufs=1))
        ps = ctx.enter_context(tc.psum_pool(name="ps", bufs=1))

        slots = sb.tile([P, J // 16], U16, name="slots")
        picks = sb.tile([P, M // 16], U16, name="picks")
        tab_s = sb.tile([P, T], U8, name="tab_s")
        late = ctx.enter_context(tc.tile_pool(name="late", bufs=1))
        zeros = late.tile([P, 3224], F32, name="zeros", offset=0)
        w_raw = late.tile([P, 4, R], F32, name="w_raw", offset=14880)
        nc.gpsimd.iota(zeros[:, :P].bitcast(I32), pattern=[[1, P]], base=0, channel_multiplier=-1)
        nc.vector.memset(tab_s[:].bitcast(I32), 0)
        warm_in = sb.tile([P, 1], F32, name="warm_in")
        warm_out = sb.tile([P, 1], F32, name="warm_out")
        nc.vector.memset(warm_in[:], 0.0)
        nc.scalar.activation(warm_out[:], warm_in[:], ACT.Silu)
        ident = sb.tile([P, P], F32, name="ident")
        nc.vector.tensor_scalar(ident[:], zeros[:, :P].bitcast(I32), 0.0, None, ALU.is_equal)
        tab_w = late.tile([P, T], I32, name="tab_w", offset=0)
        dtab_s = late.tile([P, T], U8, name="dtab_s", offset=8192)
        pw_col = sb.tile([P, 2], F32, name="pw_col")
        bias_col = late.tile([P, 1], F32, name="bias_col", offset=10240)
        gain_tile = late.tile([P, 16], F32, name="gain_tile", offset=11808)
        gain_col = gain_tile[:, 0:1]

        nc.vector.memset(dtab_s[:].bitcast(I32), 0)


        def load_scales(plane, first, scales):
            rows = scales[0].bitcast(I32).rearrange("(q r) c -> r q c", r=4)
            for r in range(4):
                nc.sync.dma_start(plane[first + r : P : 32, :].bitcast(I32), rows[r])

        def load_words(tile, words):
            nc.sync.dma_start(tile[:], words[0].rearrange("p n t -> p (n t)").bitcast(I32))

        nc.sync.dma_start(slots[:], offs)
        nc.sync.dma_start(w_raw[:], w1.rearrange("(p j) r -> p j r", j=4))
        nc.sync.dma_start(picks[:], offs2)
        load_scales(tab_s, 0, tab_scales)
        load_words(tab_w, tab_words)
        nc.sync.dma_start(bias_col[:], bias)
        nc.sync.dma_start(gain_col, gain)
        load_scales(dtab_s, 4, dtab_scales)

        nc.scalar.dma_start(pw_col[:], pw[0].rearrange("(p h) -> p h", h=2))

        w_bf = late.tile([P, R, 4], BF16, name="w_bf", align_bytes=64, offset=12864)
        nc.scalar.copy(w_bf[:], w_raw[:].rearrange("p j r -> p r j"))
        w_codes = sb.tile([P, R], U32, name="w_codes", align_bytes=64)
        w_scales = sb.tile([P, R], U8, name="w_scales", align_bytes=64)
        nc.vector.quantize_mx(out=w_codes[:].bitcast(FP8X4), scales=w_scales[:], in_=w_bf[:].rearrange("p r j -> p (r j)"))

        dtab_w = late.tile([P, T], I32, name="dtab_w", offset=14944)
        base_sb = late.tile([P, M], F32, name="base_sb", offset=13888)
        og_col = late.tile([P, 1], F32, name="og_col", offset=14912)
        load_words(dtab_w, dtab_words)
        nc.sync.dma_start(base_sb[:], base)
        nc.sync.dma_start(og_col[:], og)
        pw_ps = ps.tile([P, 2, P], F32, name="pw_ps", tag="a0")
        for h in range(2):
            nc.tensor.transpose(pw_ps[:, h, :], pw_col[:, h : h + 1].to_broadcast([P, P]), ident[:])
        pw_row = sb.tile([P, M], F32, name="pw_row")
        nc.scalar.copy(pw_row[:].rearrange("i (p h) -> i p h", h=2), pw_ps[:].rearrange("i h p -> i p h"))
        gain_neg = sb.tile([P, 1], F32, name="gain_neg")
        nc.gpsimd.tensor_scalar(gain_neg[:], gain_col, -1.0, 0.0, ALU.mult, ALU.add)
        og_neg_half = sb.tile([P, 1], F32, name="og_neg_half")
        nc.gpsimd.tensor_scalar(og_neg_half[:], og_col[:], -0.5, 0.0, ALU.mult, ALU.add)

        def gather_scales(plane, got):
            nc.vector.tensor_copy(got[:], plane[:].indirect(slots[:]))
            return got

        def product(tile, got_scales, first, h, name, got):
            nc.vector.tensor_copy(got[:], tile[:].bitcast(U32).indirect(slots[:, h * HALF // 16 : (h + 1) * HALF // 16]))
            acc = ps.tile([P, HALF], F32, name=name, tag=name)
            nc.tensor.matmul_mx(
                out=acc[:],
                lhsT=w_codes[:].bitcast(FP8X4),
                lhsT_scale=w_scales[:],
                rhs=got[:].bitcast(FP8X4),
                rhs_scale=got_scales[first:P, h * HALF : (h + 1) * HALF],
                start=True,
                stop=True,
            )
            return acc

        h1 = sb.tile([P, J], F32, name="h1")
        h2 = sb.tile([P, J], F32, name="h2")
        tab_sg = gather_scales(tab_s, late.tile([P, J], U8, name="tab_sg", align_bytes=64, offset=10304))
        for h in range(2):
            cols = slice(h * HALF, (h + 1) * HALF)
            a = product(tab_w, tab_sg, 0, h, "a%d" % h, sb.tile([P, HALF], U32, name="a_got%d" % h, align_bytes=64))
            nc.scalar.activation(h1[:, cols], a[:], ACT.Tanh, bias=bias_col[:])
            nc.scalar.activation(h2[:, cols], h1[:, cols], ACT.Copy, scale=gain_col)
        dtab_sg = gather_scales(dtab_s, sb.tile([P, J], U8, name="dtab_sg", align_bytes=64))

        s = late.tile([P, M], F32, name="s", offset=8192)
        nc.vector.tensor_tensor(s[:], h2[:].indirect(picks[:]), pw_row[:], ALU.mult)
        sq = sb.tile([P, J], F32, name="sq")
        nc.scalar.activation(sq[:], h1[:], ACT.Square)
        slope = sb.tile([P, J], F32, name="slope")
        nc.scalar.activation(slope[:], sq[:], ACT.Copy, bias=-1.0)
        silu_neg = sb.tile([P, M], F32, name="silu_neg")
        nc.scalar.activation(silu_neg[:], s[:], ACT.Silu, scale=-1.0)
        tanh_half = sb.tile([P, M], F32, name="tanh_half")
        nc.scalar.activation(tanh_half[:], s[:], ACT.Tanh, scale=0.5)

        ta = [product(dtab_w, dtab_sg, 4, h, "ta%d" % h, late.tile([P, HALF], U32, name="ta_got%d" % h, align_bytes=64, offset=10816 + 1024 * h)) for h in range(2)]
        v = late.tile([P, M], F32, name="v", offset=10816)
        nc.vector.scalar_tensor_tensor(v[:], silu_neg[:], 1.0, pw_row[:], ALU.subtract, ALU.mult)
        th2 = sb.tile([P, J], F32, name="th2")
        nc.vector.scalar_tensor_tensor(th2[:, :HALF], ta[0][:], gain_neg[:], slope[:, :HALF], ALU.mult, ALU.mult)
        factor = sb.tile([P, M], F32, name="factor")
        nc.vector.scalar_tensor_tensor(factor[:], tanh_half[:], 1.0, v[:], ALU.add, ALU.mult)
        nc.vector.scalar_tensor_tensor(th2[:, HALF:], ta[1][:], gain_neg[:], slope[:, HALF:], ALU.mult, ALU.mult)
        picked = sb.tile([P, M], F32, name="picked")
        res = sb.tile([P, M], F32, name="res")
        halves = [slice(h * M // 2, (h + 1) * M // 2) for h in range(2)]
        for h, cols in enumerate(halves):
            nc.vector.tensor_tensor(picked[:, cols], th2[:].indirect(picks[:, 8 * h : 8 * h + 8]), factor[:, cols], ALU.mult)
        for queue, cols in zip((nc.scalar, nc.sync), halves):
            nc.vector.scalar_tensor_tensor(res[:, cols], picked[:, cols], og_neg_half[:], base_sb[:, cols], ALU.mult, ALU.add)
            queue.dma_start(out[:, cols], res[:, cols])
